import numpy as np
import ml_dtypes


def mxq(x, axis, fmt="e4m3"):
    dtype, down = {"e4m3": (ml_dtypes.float8_e4m3fn, 7), "e5m2": (ml_dtypes.float8_e5m2, 14)}[fmt]
    v = np.moveaxis(np.asarray(x, np.float32).astype(ml_dtypes.bfloat16).astype(np.float64), axis, -1)
    blocks = v.reshape(v.shape[:-1] + (-1, 32))
    amax = np.abs(blocks).max(-1, keepdims=True)
    byte = np.maximum(np.where(amax > 0, np.frexp(amax)[1] - 1 + 127, 0) - down, 1)
    scale = np.exp2(byte - 127.0)
    codes = (blocks / scale).astype(np.float32).astype(dtype).astype(np.float64)
    return np.moveaxis((codes * scale).reshape(v.shape), -1, axis)


WIDE = False


def mx_kscale(k):
    if not WIDE:
        return np.ones(k)
    levels = np.array([10, -10, 5, -5, 0])
    if k % 512:
        return np.exp2(np.random.permutation(np.resize(levels, k // 32))).repeat(32)
    a = np.empty((k // 512, 16))
    for p in range(k // 512):
        a[p, :8] = np.random.permutation(np.resize(levels, 8))
        for g in range(8):
            far = levels[np.abs(levels - a[p, g]) >= 10]
            a[p, g + 8] = far[np.random.randint(len(far))]
    return np.exp2(a.ravel()).repeat(32)


def f64(x):
    return np.asarray(x).astype(np.float64)


def striped(idx):
    return np.tile(idx.reshape(-1, 16).T, (8, 1)).astype(np.uint16)


def unstriped(offs):
    return offs[:16].T.reshape(-1).astype(np.int64)


def pack_weight(w):
    k, n = w.shape
    w = f64(np.asarray(w, np.float32).astype(ml_dtypes.bfloat16)).reshape(k // 32, 32, n)
    amax = np.abs(w).max(1)
    byte = np.clip(np.where(amax > 0, np.frexp(amax)[1] - 1 + 127 - 7, 1), 1, 254)
    scaled = (w * np.exp2(127.0 - byte)[:, None, :]).reshape(k, n).astype(np.float32)
    words = np.ascontiguousarray(scaled.reshape(k // 512, 128, 4, n).transpose(0, 1, 3, 2)).astype(ml_dtypes.float8_e4m3fn).view(np.uint8)
    return words, np.ascontiguousarray(byte.astype(np.uint8).reshape(k // 512, 16, n))


def unpack_weight(words, scales):
    g, p, n, _ = words.shape
    vals = np.ascontiguousarray(words).view(ml_dtypes.float8_e4m3fn).astype(np.float64) * np.repeat(np.exp2(scales.astype(np.float64) - 127.0), 8, axis=1)[..., None]
    return vals.transpose(0, 1, 3, 2).reshape(g * 512, n)


K, T, E, C, N = 1536, 1024, 2, 256, 256


def by_expert(wq, xq):
    return np.concatenate([wq[e].T @ xq[:, e * C:(e + 1) * C] for e in range(E)], axis=1)


def setup_inputs():
    n = np.random.standard_normal
    s = mx_kscale(K)[:, None]
    packed = [pack_weight(m) for m in n((E, K, N)) / np.sqrt(K) / s[None]]
    return {
        "xT": (n((K, T)) * s).astype(np.float32),
        "w_words": np.stack([m[0] for m in packed]),
        "w_scales": np.stack([m[1] for m in packed]),
        "gate": np.tile(np.random.uniform(0.2, 1.0, E * C), (N, 1)).astype(np.float32),
        "offs": striped(np.random.permutation(T)[:E * C]),
    }


def reference(xT, w_words, w_scales, gate, offs):
    idx = unstriped(offs)
    xq = mxq(f64(xT)[:, idx], 0, "e4m3")
    w = np.stack([unpack_weight(w_words[e], w_scales[e]) for e in range(E)])
    y = by_expert(w, xq)
    out = np.zeros((N, T))
    out[:, idx] = f64(gate) * y
    return out

@@ -1,0 +1,125 @@
+from contextlib import ExitStack
+
+import concourse.mybir as mybir
+
+K, T, E, C, N = 1536, 1024, 2, 256, 256
+S = E * C
+P = 128
+PASSES = K // 512
+BLOCKS = N // P
+
+FLOPS = 2 * S * K * N
+BYTES = 4 * K * T + E * K * N + E * K * N // 32 + 4 * S + 2 * 8 * 16 * (S // 16) + 4 * N * T
+
+F32 = mybir.dt.float32
+BF16 = mybir.dt.bfloat16
+I32 = mybir.dt.int32
+U32 = mybir.dt.uint32
+U16 = mybir.dt.uint16
+U8 = mybir.dt.uint8
+FP8X4 = mybir.dt.float8_e4m3fn_x4
+MULT = mybir.AluOpType.mult
+
+WHOLE = [(0, 1024, 384)]
+LAST = [(0, 640, 384), (640, 384, 288)]
+
+
+def tile_routed_moe_kernel(tc, xT, w_words, w_scales, gate, offs, out):
+    nc = tc.nc
+    with ExitStack() as ctx:
+        keep = ctx.enter_context(tc.tile_pool(name="keep", bufs=1))
+        psum = ctx.enter_context(tc.psum_pool(name="psum", bufs=1))
+
+        offsets = keep.tile([P, S // 16], U16, name="offsets")
+        nc.sync.dma_start(offsets[:], offs)
+
+        warm = keep.tile([P, 16], F32, name="warm")
+        warm_out = keep.tile([P, 16], BF16, name="warm_out")
+        nc.vector.memset(warm[:], 0.0)
+        nc.scalar.copy(out=warm_out[:], in_=warm[:])
+
+        w_planes = keep.tile([P, E * PASSES, N], U8, name="w_planes", align_bytes=64)
+        nc.vector.memset(w_planes[:].rearrange("p a n -> p (a n)").bitcast(I32), 0)
+        windows = []
+        for b in range(BLOCKS):
+            window = keep.tile([P, T], F32, name=f"window{b}")
+            nc.vector.memset(window[:], 0.0)
+            windows.append(window)
+
+        x_rows = xT.rearrange("(g p u v) t -> g u p v t", p=P, u=2, v=2)
+        raws = []
+        for g in range(PASSES):
+            for u in range(2):
+                raw = keep.tile([P, 2, T], F32, name=f"raw{g}{u}")
+                last = g == PASSES - 1 and u == 1
+                for t0, n, v in (LAST if last else WHOLE):
+                    nc.sync.dma_start(raw[:, :, t0 : t0 + n], x_rows[g, u, :, :, t0 : t0 + n])
+                raws.append(raw)
+
+        w_codes = keep.tile([P, E, PASSES, N], U32, name="w_codes", align_bytes=64)
+        for q in range(4):
+            nc.sync.dma_start(
+                w_planes[32 * q : 32 * q + 4, :, :].bitcast(I32),
+                w_scales[:, :, 4 * q : 4 * q + 4, :].rearrange("e a q n -> q (e a) n").bitcast(I32),
+            )
+        for e in range(E):
+            nc.sync.dma_start(
+                w_codes[:, e, :, :].bitcast(I32),
+                w_words[e].rearrange("a p n r -> p a (n r)").bitcast(I32),
+            )
+        gates = keep.tile([P, S], F32, name="gates")
+        nc.sync.dma_start(gates[:], gate[0:P, :])
+
+        x_codes = keep.tile([P, PASSES, S], U32, name="x_codes", align_bytes=64)
+        x_planes = keep.tile([P, PASSES, S], U8, name="x_planes", align_bytes=64)
+        sums = []
+        for e in range(E):
+            row = []
+            for b in range(BLOCKS):
+                acc = psum.tile([P, C], F32, name=f"acc{e}{b}")
+                row.append(acc)
+            sums.append(row)
+
+        for g in range(PASSES):
+            grouped = keep.tile([P, S, 4], BF16, name=f"grouped{g}", align_bytes=64)
+            words = grouped[:].rearrange("p s r -> p (s r)").bitcast(U32).rearrange("p (s u) -> p s u", u=2)
+            last_pass = g == PASSES - 1
+            cuts = [(0, C), (C, C)] if last_pass else [(0, S)]
+            for u in range(2):
+                raw = raws[2 * g + u]
+                pairs = keep.tile([P, T, 2], BF16, name=f"pairs{g}{u}")
+                for t0, n, v in (LAST if last_pass and u == 1 else WHOLE):
+                    src = raw[:].rearrange("p v t -> p t v")
+                    nc.vector.tensor_copy(out=pairs[:, t0 : t0 + v, :], in_=src[:, t0 : t0 + v, :])
+                    nc.scalar.copy(out=pairs[:, t0 + v : t0 + n, :], in_=src[:, t0 + v : t0 + n, :])
+                window = pairs[:].rearrange("p t v -> p (t v)").bitcast(U32)
+                for s0, n in cuts:
+                    nc.vector.tensor_copy(
+                        out=words[:, s0 : s0 + n, u],
+                        in_=window.indirect(offsets[:, s0 // 16 : (s0 + n) // 16]),
+                    )
+            for s0, n in cuts:
+                nc.vector.quantize_mx(
+                    out=x_codes[:, g, s0 : s0 + n].bitcast(FP8X4),
+                    scales=x_planes[:, g, s0 : s0 + n],
+                    in_=grouped[:, s0 : s0 + n, :].rearrange("p s r -> p (s r)"),
+                )
+            for e in range(E):
+                for b in range(BLOCKS):
+                    nc.tensor.matmul_mx(
+                        out=sums[e][b][:],
+                        lhsT=w_codes[:, e, g, b * P : (b + 1) * P].bitcast(FP8X4),
+                        lhsT_scale=w_planes[:, e * PASSES + g, b * P : (b + 1) * P],
+                        rhs=x_codes[:, g, e * C : (e + 1) * C].bitcast(FP8X4),
+                        rhs_scale=x_planes[:, g, e * C : (e + 1) * C],
+                        start=(g == 0),
+                        stop=last_pass,
+                    )
+
+        for b in range(BLOCKS):
+            gated = keep.tile([P, S], F32, name=f"gated{b}")
+            for e in range(E):
+                cols = slice(e * C, (e + 1) * C)
+                nc.vector.tensor_tensor(out=gated[:, cols], in0=sums[e][b][:], in1=gates[:, cols], op=MULT)
+            nc.vector.tensor_copy(out=windows[b][:].indirect(offsets[:]), in_=gated[:])
+            nc.sync.dma_start(out[b * P : (b + 1) * P, :], windows[b][:])

@@ -20,24 +20,29 @@ U8 = mybir.dt.uint8
 FP8X4 = mybir.dt.float8_e4m3fn_x4
 MULT = mybir.AluOpType.mult
 
-WHOLE = [(0, 1024, 384)]
-LAST = [(0, 640, 384), (640, 384, 288)]
+LOADS = [[(0, 256), (256, 256), (512, 512)], [(0, 512), (512, 512)], [(0, 512), (512, 256), (768, 256)]]
+CASTS = [[(0, 256, 96), (256, 256, 192), (512, 512, 480)], [(0, 512, 32), (512, 512, 256)], [(0, 512, 256), (512, 256, 96), (768, 256, 96)]]
+PLANE = [(0, 0), (1, 0), (1, 4)]
+CUTS = [[(0, S)], [(0, S)], [(0, C), (C, C)]]
 
 
 def tile_routed_moe_kernel(tc, xT, w_words, w_scales, gate, offs, out):
     nc = tc.nc
     with ExitStack() as ctx:
         keep = ctx.enter_context(tc.tile_pool(name="keep", bufs=1))
+        ring = ctx.enter_context(tc.tile_pool(name="ring", bufs=3))
         psum = ctx.enter_context(tc.psum_pool(name="psum", bufs=1))
-
-        offsets = keep.tile([P, S // 16], U16, name="offsets")
-        nc.sync.dma_start(offsets[:], offs)
 
         warm = keep.tile([P, 16], F32, name="warm")
         warm_out = keep.tile([P, 16], BF16, name="warm_out")
         nc.vector.memset(warm[:], 0.0)
         nc.scalar.copy(out=warm_out[:], in_=warm[:])
 
+        planes = []
+        for i in range(2):
+            plane = keep.tile([P, T], U8, name=f"plane{i}", align_bytes=64)
+            nc.gpsimd.memset(plane[:], 0)
+            planes.append(plane)
         w_planes = keep.tile([P, E * PASSES, N], U8, name="w_planes", align_bytes=64)
         nc.vector.memset(w_planes[:].rearrange("p a n -> p (a n)").bitcast(I32), 0)
         windows = []
@@ -46,15 +51,16 @@ def tile_routed_moe_kernel(tc, xT, w_words, w_scales, gate, offs, out):
             nc.vector.memset(window[:], 0.0)
             windows.append(window)
 
-        x_rows = xT.rearrange("(g p u v) t -> g u p v t", p=P, u=2, v=2)
+        x_rows = xT.rearrange("(g p r) t -> g p r t", p=P, r=4)
         raws = []
+        offsets = keep.tile([P, S // 16], U16, name="offsets")
         for g in range(PASSES):
-            for u in range(2):
-                raw = keep.tile([P, 2, T], F32, name=f"raw{g}{u}")
-                last = g == PASSES - 1 and u == 1
-                for t0, n, v in (LAST if last else WHOLE):
-                    nc.sync.dma_start(raw[:, :, t0 : t0 + n], x_rows[g, u, :, :, t0 : t0 + n])
-                raws.append(raw)
+            for t0, n in LOADS[g]:
+                raw = keep.tile([P, 4, n], F32, name=f"raw{g}_{t0}")
+                nc.sync.dma_start(raw[:], x_rows[g, :, :, t0 : t0 + n])
+                raws.append((g, t0, n, raw))
+            if g == 0:
+                nc.sync.dma_start(offsets[:], offs)
 
         w_codes = keep.tile([P, E, PASSES, N], U32, name="w_codes", align_bytes=64)
         for q in range(4):
@@ -71,7 +77,7 @@ def tile_routed_moe_kernel(tc, xT, w_words, w_scales, gate, offs, out):
         nc.sync.dma_start(gates[:], gate[0:P, :])
 
         x_codes = keep.tile([P, PASSES, S], U32, name="x_codes", align_bytes=64)
-        x_planes = keep.tile([P, PASSES, S], U8, name="x_planes", align_bytes=64)
+        x_planes = keep.tile([P, 2, S], U8, name="x_planes", align_bytes=64)
         sums = []
         for e in range(E):
             row = []
@@ -81,45 +87,55 @@ def tile_routed_moe_kernel(tc, xT, w_words, w_scales, gate, offs, out):
             sums.append(row)
 
         for g in range(PASSES):
-            grouped = keep.tile([P, S, 4], BF16, name=f"grouped{g}", align_bytes=64)
-            words = grouped[:].rearrange("p s r -> p (s r)").bitcast(U32).rearrange("p (s u) -> p s u", u=2)
-            last_pass = g == PASSES - 1
-            cuts = [(0, C), (C, C)] if last_pass else [(0, S)]
-            for u in range(2):
-                raw = raws[2 * g + u]
-                pairs = keep.tile([P, T, 2], BF16, name=f"pairs{g}{u}")
-                for t0, n, v in (LAST if last_pass and u == 1 else WHOLE):
-                    src = raw[:].rearrange("p v t -> p t v")
-                    nc.vector.tensor_copy(out=pairs[:, t0 : t0 + v, :], in_=src[:, t0 : t0 + v, :])
-                    nc.scalar.copy(out=pairs[:, t0 + v : t0 + n, :], in_=src[:, t0 + v : t0 + n, :])
-                window = pairs[:].rearrange("p t v -> p (t v)").bitcast(U32)
-                for s0, n in cuts:
-                    nc.vector.tensor_copy(
-                        out=words[:, s0 : s0 + n, u],
-                        in_=window.indirect(offsets[:, s0 // 16 : (s0 + n) // 16]),
-                    )
-            for s0, n in cuts:
+            codes = keep.tile([P, T], U32, name=f"codes{g}", align_bytes=64)
+            i, k = PLANE[g]
+            for t0, n, v in CASTS[g]:
+                grouped = ring.tile([P, n, 4], BF16, name="grouped", align_bytes=64)
+                dst = grouped[:].rearrange("p (c i) r -> p c r i", i=4)
+                start, raw = [(l0, tile) for lg, l0, ln, tile in raws if lg == g and l0 <= t0 < l0 + ln][0]
+                src = raw[:].rearrange("p r (c i) -> p c r i", i=4)
+                c0, c1, c2 = 0, v // 4, n // 4
+                o = (t0 - start) // 4
+                if v:
+                    nc.vector.tensor_copy(out=dst[:, 0 : c1 - c0], in_=src[:, o + c0 : o + c1])
+                if v < n:
+                    nc.scalar.copy(out=dst[:, c1 - c0 : c2 - c0], in_=src[:, o + c1 : o + c2])
                 nc.vector.quantize_mx(
-                    out=x_codes[:, g, s0 : s0 + n].bitcast(FP8X4),
-                    scales=x_planes[:, g, s0 : s0 + n],
-                    in_=grouped[:, s0 : s0 + n, :].rearrange("p s r -> p (s r)"),
+                    out=codes[:, t0 : t0 + n].bitcast(FP8X4),
+                    scales=planes[i][k:P, t0 : t0 + n],
+                    in_=grouped[:].rearrange("p t r -> p (t r)"),
                 )
+            for s0, n in CUTS[g]:
+                entries = offsets[:, s0 // 16 : (s0 + n) // 16]
+                nc.vector.tensor_copy(out=x_codes[:, g, s0 : s0 + n], in_=codes[:].indirect(entries))
+                if g != 1:
+                    nc.vector.tensor_copy(out=x_planes[:, i, s0 : s0 + n], in_=planes[i][:].indirect(entries))
             for e in range(E):
                 for b in range(BLOCKS):
-                    nc.tensor.matmul_mx(
-                        out=sums[e][b][:],
-                        lhsT=w_codes[:, e, g, b * P : (b + 1) * P].bitcast(FP8X4),
-                        lhsT_scale=w_planes[:, e * PASSES + g, b * P : (b + 1) * P],
-                        rhs=x_codes[:, g, e * C : (e + 1) * C].bitcast(FP8X4),
-                        rhs_scale=x_planes[:, g, e * C : (e + 1) * C],
-                        start=(g == 0),
-                        stop=last_pass,
-                    )
+                    for a in ([0], [], [1, 2])[g]:
+                        ia, ka = PLANE[a]
+                        nc.tensor.matmul_mx(
+                            out=sums[e][b][:],
+                            lhsT=w_codes[:, e, a, b * P : (b + 1) * P].bitcast(FP8X4),
+                            lhsT_scale=w_planes[:, e * PASSES + a, b * P : (b + 1) * P],
+                            rhs=x_codes[:, a, e * C : (e + 1) * C].bitcast(FP8X4),
+                            rhs_scale=x_planes[ka:P, ia, e * C : (e + 1) * C],
+                            start=(a == 0),
+                            stop=(a == PASSES - 1),
+                        )
 
+        ys = {}
+        for e in range(E):
+            for b in range(BLOCKS):
+                y = keep.tile([P, C], F32, name=f"y{e}{b}")
+                nc.scalar.copy(out=y[:], in_=sums[e][b][:])
+                ys[e, b] = y
         for b in range(BLOCKS):
-            gated = keep.tile([P, S], F32, name=f"gated{b}")
             for e in range(E):
-                cols = slice(e * C, (e + 1) * C)
-                nc.vector.tensor_tensor(out=gated[:, cols], in0=sums[e][b][:], in1=gates[:, cols], op=MULT)
-            nc.vector.tensor_copy(out=windows[b][:].indirect(offsets[:]), in_=gated[:])
+                nc.vector.tensor_tensor(
+                    out=windows[b][:].indirect(offsets[:, e * C // 16 : (e + 1) * C // 16]),
+                    in0=ys[e, b][:],
+                    in1=gates[:, e * C : (e + 1) * C],
+                    op=MULT,
+                )
             nc.sync.dma_start(out[b * P : (b + 1) * P, :], windows[b][:])

@@ -20,10 +20,8 @@ U8 = mybir.dt.uint8
 FP8X4 = mybir.dt.float8_e4m3fn_x4
 MULT = mybir.AluOpType.mult
 
-LOADS = [[(0, 256), (256, 256), (512, 512)], [(0, 512), (512, 512)], [(0, 512), (512, 256), (768, 256)]]
-CASTS = [[(0, 256, 96), (256, 256, 192), (512, 512, 480)], [(0, 512, 32), (512, 512, 256)], [(0, 512, 256), (512, 256, 96), (768, 256, 96)]]
-PLANE = [(0, 0), (1, 0), (1, 4)]
-CUTS = [[(0, S)], [(0, S)], [(0, C), (C, C)]]
+LOADS = [[(0, 1024)], [(0, 1024)], [(0, 512), (512, 256), (768, 256)]]
+CASTS = [[(0, 512, 288), (512, 512, 352)], [(0, 512, 384), (512, 512, 224)], [(0, 512, 192), (512, 256, 32), (768, 256, 128)]]
 
 
 def tile_routed_moe_kernel(tc, xT, w_words, w_scales, gate, offs, out):
@@ -38,11 +36,8 @@ def tile_routed_moe_kernel(tc, xT, w_words, w_scales, gate, offs, out):
         nc.vector.memset(warm[:], 0.0)
         nc.scalar.copy(out=warm_out[:], in_=warm[:])
 
-        planes = []
-        for i in range(2):
-            plane = keep.tile([P, T], U8, name=f"plane{i}", align_bytes=64)
-            nc.gpsimd.memset(plane[:], 0)
-            planes.append(plane)
+        planes = keep.tile([P, T], U8, name="planes", align_bytes=64)
+        nc.gpsimd.memset(planes[:], 0)
         w_planes = keep.tile([P, E * PASSES, N], U8, name="w_planes", align_bytes=64)
         nc.vector.memset(w_planes[:].rearrange("p a n -> p (a n)").bitcast(I32), 0)
         windows = []
@@ -77,58 +72,57 @@ def tile_routed_moe_kernel(tc, xT, w_words, w_scales, gate, offs, out):
         nc.sync.dma_start(gates[:], gate[0:P, :])
 
         x_codes = keep.tile([P, PASSES, S], U32, name="x_codes", align_bytes=64)
-        x_planes = keep.tile([P, 2, S], U8, name="x_planes", align_bytes=64)
-        sums = []
+        x_planes = keep.tile([P, S], U8, name="x_planes", align_bytes=64)
+        sums = {}
         for e in range(E):
-            row = []
             for b in range(BLOCKS):
                 acc = psum.tile([P, C], F32, name=f"acc{e}{b}")
-                row.append(acc)
-            sums.append(row)
+                sums[e, b] = acc
 
         for g in range(PASSES):
             codes = keep.tile([P, T], U32, name=f"codes{g}", align_bytes=64)
-            i, k = PLANE[g]
             for t0, n, v in CASTS[g]:
                 grouped = ring.tile([P, n, 4], BF16, name="grouped", align_bytes=64)
+                first, raw = [(l0, tile) for lg, l0, ln, tile in raws if lg == g and l0 <= t0 < l0 + ln][0]
+                o = t0 - first
                 dst = grouped[:].rearrange("p (c i) r -> p c r i", i=4)
-                start, raw = [(l0, tile) for lg, l0, ln, tile in raws if lg == g and l0 <= t0 < l0 + ln][0]
-                src = raw[:].rearrange("p r (c i) -> p c r i", i=4)
-                c0, c1, c2 = 0, v // 4, n // 4
-                o = (t0 - start) // 4
+                src = raw[:, :, o : o + n].rearrange("p r (c i) -> p c r i", i=4)
+                c = v // 4
                 if v:
-                    nc.vector.tensor_copy(out=dst[:, 0 : c1 - c0], in_=src[:, o + c0 : o + c1])
+                    nc.vector.tensor_copy(out=dst[:, :c], in_=src[:, :c])
                 if v < n:
-                    nc.scalar.copy(out=dst[:, c1 - c0 : c2 - c0], in_=src[:, o + c1 : o + c2])
+                    nc.scalar.copy(out=dst[:, c:], in_=src[:, c:])
                 nc.vector.quantize_mx(
                     out=codes[:, t0 : t0 + n].bitcast(FP8X4),
-                    scales=planes[i][k:P, t0 : t0 + n],
+                    scales=planes[4 * g : P, t0 : t0 + n],
                     in_=grouped[:].rearrange("p t r -> p (t r)"),
                 )
-            for s0, n in CUTS[g]:
-                entries = offsets[:, s0 // 16 : (s0 + n) // 16]
-                nc.vector.tensor_copy(out=x_codes[:, g, s0 : s0 + n], in_=codes[:].indirect(entries))
-                if g != 1:
-                    nc.vector.tensor_copy(out=x_planes[:, i, s0 : s0 + n], in_=planes[i][:].indirect(entries))
-            for e in range(E):
-                for b in range(BLOCKS):
-                    for a in ([0], [], [1, 2])[g]:
-                        ia, ka = PLANE[a]
-                        nc.tensor.matmul_mx(
-                            out=sums[e][b][:],
-                            lhsT=w_codes[:, e, a, b * P : (b + 1) * P].bitcast(FP8X4),
-                            lhsT_scale=w_planes[:, e * PASSES + a, b * P : (b + 1) * P],
-                            rhs=x_codes[:, a, e * C : (e + 1) * C].bitcast(FP8X4),
-                            rhs_scale=x_planes[ka:P, ia, e * C : (e + 1) * C],
-                            start=(a == 0),
-                            stop=(a == PASSES - 1),
-                        )
+            if g < PASSES - 1:
+                nc.vector.tensor_copy(out=x_codes[:, g, :], in_=codes[:].indirect(offsets[:]))
+            else:
+                for e in range(E):
+                    cols = slice(e * C, (e + 1) * C)
+                    entries = offsets[:, e * C // 16 : (e + 1) * C // 16]
+                    nc.vector.tensor_copy(out=x_planes[:, cols], in_=planes[:].indirect(entries))
+                    nc.vector.tensor_copy(out=x_codes[:, g, cols], in_=codes[:].indirect(entries))
 
         ys = {}
         for e in range(E):
+            cols = slice(e * C, (e + 1) * C)
             for b in range(BLOCKS):
+                rows = slice(b * P, (b + 1) * P)
+                for g in range(PASSES):
+                    nc.tensor.matmul_mx(
+                        out=sums[e, b][:],
+                        lhsT=w_codes[:, e, g, rows].bitcast(FP8X4),
+                        lhsT_scale=w_planes[:, e * PASSES + g, rows],
+                        rhs=x_codes[:, g, cols].bitcast(FP8X4),
+                        rhs_scale=x_planes[4 * g : P, cols],
+                        start=(g == 0),
+                        stop=(g == PASSES - 1),
+                    )
                 y = keep.tile([P, C], F32, name=f"y{e}{b}")
-                nc.scalar.copy(out=y[:], in_=sums[e][b][:])
+                nc.scalar.copy(out=y[:], in_=sums[e, b][:])
                 ys[e, b] = y
         for b in range(BLOCKS):
             for e in range(E):

from contextlib import ExitStack

import concourse.mybir as mybir

K, T, E, C, N = 1536, 1024, 2, 256, 256
S = E * C
P = 128
PASSES = K // 512
BLOCKS = N // P

FLOPS = 2 * S * K * N
BYTES = 4 * K * T + E * K * N + E * K * N // 32 + 4 * S + 2 * 8 * 16 * (S // 16) + 4 * N * T

F32 = mybir.dt.float32
BF16 = mybir.dt.bfloat16
I32 = mybir.dt.int32
U32 = mybir.dt.uint32
U16 = mybir.dt.uint16
U8 = mybir.dt.uint8
FP8X4 = mybir.dt.float8_e4m3fn_x4
MULT = mybir.AluOpType.mult

LOADS = [[(0, 1024)], [(0, 1024)], [(0, 512), (512, 256), (768, 256)]]
CASTS = [[(0, 512, 288), (512, 512, 352)], [(0, 512, 384), (512, 512, 224)], [(0, 512, 192), (512, 256, 32), (768, 256, 128)]]


def tile_routed_moe_kernel(tc, xT, w_words, w_scales, gate, offs, out):
    nc = tc.nc
    with ExitStack() as ctx:
        keep = ctx.enter_context(tc.tile_pool(name="keep", bufs=1))
        ring = ctx.enter_context(tc.tile_pool(name="ring", bufs=3))
        psum = ctx.enter_context(tc.psum_pool(name="psum", bufs=1))

        warm = keep.tile([P, 16], F32, name="warm")
        warm_out = keep.tile([P, 16], BF16, name="warm_out")
        nc.vector.memset(warm[:], 0.0)
        nc.scalar.copy(out=warm_out[:], in_=warm[:])

        planes = keep.tile([P, T], U8, name="planes", align_bytes=64)
        nc.gpsimd.memset(planes[:], 0)
        w_planes = keep.tile([P, E * PASSES, N], U8, name="w_planes", align_bytes=64)
        nc.vector.memset(w_planes[:].rearrange("p a n -> p (a n)").bitcast(I32), 0)
        windows = []
        for b in range(BLOCKS):
            window = keep.tile([P, T], F32, name=f"window{b}")
            nc.vector.memset(window[:], 0.0)
            windows.append(window)

        x_rows = xT.rearrange("(g p r) t -> g p r t", p=P, r=4)
        raws = []
        offsets = keep.tile([P, S // 16], U16, name="offsets")
        for g in range(PASSES):
            for t0, n in LOADS[g]:
                raw = keep.tile([P, 4, n], F32, name=f"raw{g}_{t0}")
                nc.sync.dma_start(raw[:], x_rows[g, :, :, t0 : t0 + n])
                raws.append((g, t0, n, raw))
            if g == 0:
                nc.sync.dma_start(offsets[:], offs)

        w_codes = keep.tile([P, E, PASSES, N], U32, name="w_codes", align_bytes=64)
        for q in range(4):
            nc.sync.dma_start(
                w_planes[32 * q : 32 * q + 4, :, :].bitcast(I32),
                w_scales[:, :, 4 * q : 4 * q + 4, :].rearrange("e a q n -> q (e a) n").bitcast(I32),
            )
        for e in range(E):
            nc.sync.dma_start(
                w_codes[:, e, :, :].bitcast(I32),
                w_words[e].rearrange("a p n r -> p a (n r)").bitcast(I32),
            )
        gates = keep.tile([P, S], F32, name="gates")
        nc.sync.dma_start(gates[:], gate[0:P, :])

        x_codes = keep.tile([P, PASSES, S], U32, name="x_codes", align_bytes=64)
        x_planes = keep.tile([P, S], U8, name="x_planes", align_bytes=64)
        sums = {}
        for e in range(E):
            for b in range(BLOCKS):
                acc = psum.tile([P, C], F32, name=f"acc{e}{b}")
                sums[e, b] = acc

        for g in range(PASSES):
            codes = keep.tile([P, T], U32, name=f"codes{g}", align_bytes=64)
            for t0, n, v in CASTS[g]:
                grouped = ring.tile([P, n, 4], BF16, name="grouped", align_bytes=64)
                first, raw = [(l0, tile) for lg, l0, ln, tile in raws if lg == g and l0 <= t0 < l0 + ln][0]
                o = t0 - first
                dst = grouped[:].rearrange("p (c i) r -> p c r i", i=4)
                src = raw[:, :, o : o + n].rearrange("p r (c i) -> p c r i", i=4)
                c = v // 4
                if v:
                    nc.vector.tensor_copy(out=dst[:, :c], in_=src[:, :c])
                if v < n:
                    nc.scalar.copy(out=dst[:, c:], in_=src[:, c:])
                nc.vector.quantize_mx(
                    out=codes[:, t0 : t0 + n].bitcast(FP8X4),
                    scales=planes[4 * g : P, t0 : t0 + n],
                    in_=grouped[:].rearrange("p t r -> p (t r)"),
                )
            if g < PASSES - 1:
                nc.vector.tensor_copy(out=x_codes[:, g, :], in_=codes[:].indirect(offsets[:]))
            else:
                for e in range(E):
                    cols = slice(e * C, (e + 1) * C)
                    entries = offsets[:, e * C // 16 : (e + 1) * C // 16]
                    nc.vector.tensor_copy(out=x_planes[:, cols], in_=planes[:].indirect(entries))
                    nc.vector.tensor_copy(out=x_codes[:, g, cols], in_=codes[:].indirect(entries))

        ys = {}
        for e in range(E):
            cols = slice(e * C, (e + 1) * C)
            for b in range(BLOCKS):
                rows = slice(b * P, (b + 1) * P)
                for g in range(PASSES):
                    nc.tensor.matmul_mx(
                        out=sums[e, b][:],
                        lhsT=w_codes[:, e, g, rows].bitcast(FP8X4),
                        lhsT_scale=w_planes[:, e * PASSES + g, rows],
                        rhs=x_codes[:, g, cols].bitcast(FP8X4),
                        rhs_scale=x_planes[4 * g : P, cols],
                        start=(g == 0),
                        stop=(g == PASSES - 1),
                    )
                y = keep.tile([P, C], F32, name=f"y{e}{b}")
                nc.scalar.copy(out=y[:], in_=sums[e, b][:])
                ys[e, b] = y
        for b in range(BLOCKS):
            for e in range(E):
                nc.vector.tensor_tensor(
                    out=windows[b][:].indirect(offsets[:, e * C // 16 : (e + 1) * C // 16]),
                    in0=ys[e, b][:],
                    in1=gates[:, e * C : (e + 1) * C],
                    op=MULT,
                )
            nc.sync.dma_start(out[b * P : (b + 1) * P, :], windows[b][:])
